import numpy as np
import ml_dtypes


def mxq(x, axis, fmt="e4m3"):
    dtype, down = {"e4m3": (ml_dtypes.float8_e4m3fn, 7), "e5m2": (ml_dtypes.float8_e5m2, 14)}[fmt]
    v = np.moveaxis(np.asarray(x, np.float32).astype(ml_dtypes.bfloat16).astype(np.float64), axis, -1)
    blocks = v.reshape(v.shape[:-1] + (-1, 32))
    amax = np.abs(blocks).max(-1, keepdims=True)
    byte = np.maximum(np.where(amax > 0, np.frexp(amax)[1] - 1 + 127, 0) - down, 1)
    scale = np.exp2(byte - 127.0)
    codes = (blocks / scale).astype(np.float32).astype(dtype).astype(np.float64)
    return np.moveaxis((codes * scale).reshape(v.shape), -1, axis)


WIDE = False


def mx_kscale(k):
    if not WIDE:
        return np.ones(k)
    levels = np.array([30, -30])
    if k % 512:
        return np.exp2(np.random.permutation(np.resize(levels, k // 32))).repeat(32)
    a = np.empty((k // 512, 16))
    for p in range(k // 512):
        a[p, :8] = np.random.permutation(np.resize(levels, 8))
        for g in range(8):
            far = levels[np.abs(levels - a[p, g]) >= 10]
            a[p, g + 8] = far[np.random.randint(len(far))]
    return np.exp2(a.ravel()).repeat(32)


def f64(x):
    return np.asarray(x).astype(np.float64)


def striped(idx):
    return np.tile(np.asarray(idx).reshape(-1, 16).T, (8, 1)).astype(np.uint16)


def unstriped(offs):
    return offs[:16].T.reshape(-1).astype(np.int64)


def bf(x):
    return np.asarray(x, np.float32).astype(ml_dtypes.bfloat16)


def planes(Y):
    r, m = Y.shape
    b = f64(bf(Y)).reshape(r // 32, 32, m)
    amax = np.abs(b).max(1)
    byte = np.clip(np.where(amax > 0, np.frexp(amax)[1] - 1 + 127 - 7, 1), 1, 254)
    codes = (b * np.exp2(127.0 - byte)[:, None, :]).reshape(r, m).astype(np.float32).astype(ml_dtypes.float8_e4m3fn).view(np.uint8)
    words = codes.reshape(r // 512, 128, 4, m).transpose(0, 1, 3, 2)
    return np.ascontiguousarray(words), np.ascontiguousarray(byte.astype(np.uint8).reshape(r // 512, 16, m))


T, K, R, J = 1024, 512, 2048, 512


def setup_inputs():
    n = np.random.standard_normal
    idx = np.random.permutation(R)[:J]
    ft = mx_kscale(T)
    return {
        "xt": (n((T, K)) * ft[:, None]).astype(np.float32),
        "gh": (n((T, R)) * np.exp(0.5 * n((T, 1))) / ft[:, None]).astype(np.float32),
        "mom": (1.0 * n((K, R))).astype(np.float32),
        "lr": (np.random.uniform(0.01, 0.05, (K, 1))).astype(np.float32),
        "offs": striped(idx),
    }


def reference(xt, gh, mom, lr, offs):
    idx = unstriped(offs)
    xtq = mxq(f64(xt), 0, "e4m3")
    ghidxq = mxq(f64(gh)[:, idx], 0, "e5m2")
    w = xtq.T @ ghidxq
    y = 0.9 * f64(mom)[:, idx] - f64(lr) * w
    words, scales = planes(y)
    return y, words, scales

@@ -1,0 +1,131 @@
+from contextlib import ExitStack
+
+import concourse.mybir as mybir
+
+T, K, R, J = 1024, 512, 2048, 512
+FLOPS = 2 * T * K * J
+
+F32 = mybir.dt.float32
+BF16 = mybir.dt.bfloat16
+I32 = mybir.dt.int32
+U32 = mybir.dt.uint32
+U16 = mybir.dt.uint16
+U8 = mybir.dt.uint8
+E4M3X4 = mybir.dt.float8_e4m3fn_x4
+E5M2X4 = mybir.dt.float8_e5m2_x4
+COPY = mybir.ActivationFunctionType.Copy
+ADD = mybir.AluOpType.add
+MULT = mybir.AluOpType.mult
+
+P = 128
+PACK = 4
+PASS = P * PACK
+PASSES = T // PASS
+HALF = J // 2
+DECAY = 0.9
+
+
+def tile_list_hot_neuron_wgrad_pl_kernel(tc, xt, gh, mom, lr, offs, out_0, out_1, out_2):
+    nc = tc.nc
+    with ExitStack() as ctx:
+        keep = ctx.enter_context(tc.tile_pool(name="keep", bufs=1))
+        psum = ctx.enter_context(tc.psum_pool(name="psum", bufs=1))
+
+        offsets = keep.tile([P, J // 16], U16, name="offsets")
+        nc.sync.dma_start(offsets[:], offs)
+        lr_sb = keep.tile([P, PACK], F32, name="lr_sb")
+        nc.sync.dma_start(out=lr_sb[:], in_=lr.rearrange("(p i) o -> p (i o)", i=PACK))
+
+        xt_v = xt.rearrange("(a p i) k -> a p i k", p=P, i=PACK)
+        gh_v = gh.rearrange("(a p i) r -> a p i r", p=P, i=PACK)
+        mom_v = mom.rearrange("(p i) r -> p i r", i=PACK)
+        y_v = out_0.rearrange("(p i) j -> p i j", i=PACK)
+
+        x_raw = [keep.tile([P, PACK, K], F32, name="x_raw%d" % a) for a in range(PASSES)]
+        g_raw = [[keep.tile([P, R], F32, name="g_raw%d_%d" % (a, i)) for i in range(PACK)] for a in range(PASSES)]
+        m_raw = [keep.tile([P, R], F32, name="m_raw%d" % i) for i in range(PACK)]
+        for a in range(PASSES):
+            nc.sync.dma_start(out=x_raw[a][:], in_=xt_v[a])
+            for i in range(PACK):
+                nc.sync.dma_start(out=g_raw[a][i][:], in_=gh_v[a, :, i, :])
+        for i in range(PACK):
+            nc.sync.dma_start(out=m_raw[i][:], in_=mom_v[:, i, :])
+
+        step = keep.tile([P, PACK], F32, name="step")
+        nc.vector.tensor_scalar(step[:], lr_sb[:], -1.0 / DECAY, None, MULT)
+
+        acc = [psum.tile([P, J], F32, name="acc%d" % i) for i in range(PACK)]
+        for a in range(PASSES):
+            x_bf = keep.tile([P, PACK, P, PACK], BF16, name="x_bf%d" % a, align_bytes=64)
+            nc.scalar.copy(
+                out=x_bf[:].rearrange("p s m i -> p m s i"),
+                in_=x_raw[a][:].rearrange("p i (m s) -> p m s i", s=PACK),
+            )
+            g_bf = keep.tile([P, J, PACK], BF16, name="g_bf%d" % a, align_bytes=64)
+            for i in range(PACK):
+                nc.vector.tensor_copy(g_bf[:, :, i], g_raw[a][i][:].indirect(offsets[:]))
+            x_codes = keep.tile([P, K], U32, name="x_codes%d" % a, align_bytes=64)
+            x_scales = keep.tile([P, K], U8, name="x_scales%d" % a, align_bytes=64)
+            nc.vector.quantize_mx(
+                out=x_codes[:].bitcast(E4M3X4), scales=x_scales[:], in_=x_bf[:].rearrange("p s m i -> p (s m i)")
+            )
+            g_codes = keep.tile([P, J], U32, name="g_codes%d" % a, align_bytes=64)
+            g_scales = keep.tile([P, J], U8, name="g_scales%d" % a, align_bytes=64)
+            nc.vector.quantize_mx(
+                out=g_codes[:].bitcast(E5M2X4), scales=g_scales[:], in_=g_bf[:].rearrange("p j i -> p (j i)")
+            )
+            for s in range(PACK):
+                cols = slice(s * P, (s + 1) * P)
+                nc.tensor.matmul_mx(
+                    out=acc[s][:],
+                    lhsT=x_codes[:, cols].bitcast(E4M3X4),
+                    lhsT_scale=x_scales[:, cols],
+                    rhs=g_codes[:].bitcast(E5M2X4),
+                    rhs_scale=g_scales[:],
+                    start=(a == 0),
+                    stop=(a == PASSES - 1),
+                )
+
+        upd = keep.tile([P, PACK, J], F32, name="upd")
+        for s in range(PACK):
+            nc.scalar.activation(upd[:, s, :], acc[s][:], COPY, scale=step[:, s : s + 1])
+
+        mixed = keep.tile([P, PACK, J], F32, name="mixed")
+        y = keep.tile([P, PACK, J], F32, name="y")
+        y_bf = [keep.tile([P, HALF, PACK], BF16, name="y_bf%d" % h, align_bytes=64) for h in range(2)]
+        y_codes = keep.tile([P, J], U32, name="y_codes", align_bytes=64)
+        y_scales = keep.tile([P, J], U8, name="y_scales", align_bytes=64)
+        halves = [slice(h * HALF, (h + 1) * HALF) for h in range(2)]
+        lists = [offsets[:, h * HALF // 16 : (h + 1) * HALF // 16] for h in range(2)]
+
+        def pair_in(first, h):
+            return mixed[:, first : first + 2, halves[h]].rearrange("p i j -> p j i")
+
+        for s in range(PACK - 1):
+            nc.vector.tensor_tensor(mixed[:, s, :], m_raw[s][:].indirect(offsets[:]), upd[:, s, :], ADD)
+            nc.scalar.activation(y[:, s, :], mixed[:, s, :], COPY, scale=DECAY)
+            nc.sync.dma_start(out=y_v[:, s, :], in_=y[:, s, :])
+            if s == 1:
+                for h in range(2):
+                    nc.scalar.activation(y_bf[h][:, :, 0:2], pair_in(0, h), COPY, scale=DECAY)
+        last = PACK - 1
+        for h in range(2):
+            nc.vector.tensor_tensor(
+                mixed[:, last, halves[h]], m_raw[last][:].indirect(lists[h]), upd[:, last, halves[h]], ADD
+            )
+        nc.scalar.activation(y_bf[0][:, :, 2:4], pair_in(2, 0), COPY, scale=DECAY)
+        nc.vector.tensor_scalar(y_bf[1][:, :, 2:4], pair_in(2, 1), DECAY, None, MULT)
+        nc.scalar.activation(y[:, last, :], mixed[:, last, :], COPY, scale=DECAY)
+        nc.sync.dma_start(out=y_v[:, last, :], in_=y[:, last, :])
+        words = out_1[0].rearrange("p c r -> p (c r)").bitcast(I32)
+        for h in range(2):
+            nc.vector.quantize_mx(
+                out=y_codes[:, halves[h]].bitcast(E4M3X4),
+                scales=y_scales[:, halves[h]],
+                in_=y_bf[h][:].rearrange("p j i -> p (j i)"),
+            )
+            nc.sync.dma_start(out=words[:, halves[h]], in_=y_codes[:, halves[h]].bitcast(I32))
+        scale_rows = out_2[0].bitcast(I32)
+        for q in range(4):
+            queue = nc.scalar if q % 2 == 0 else nc.sync
+            queue.dma_start(out=scale_rows[4 * q : 4 * q + 4, :], in_=y_scales[32 * q : 32 * q + 4, :].bitcast(I32))

@@ -22,6 +22,7 @@ PACK = 4
 PASS = P * PACK
 PASSES = T // PASS
 HALF = J // 2
+QUARTER = J // 4
 DECAY = 0.9
 
 
@@ -32,9 +33,7 @@ def tile_list_hot_neuron_wgrad_pl_kernel(tc, xt, gh, mom, lr, offs, out_0, out_1
         psum = ctx.enter_context(tc.psum_pool(name="psum", bufs=1))
 
         offsets = keep.tile([P, J // 16], U16, name="offsets")
-        nc.sync.dma_start(offsets[:], offs)
         lr_sb = keep.tile([P, PACK], F32, name="lr_sb")
-        nc.sync.dma_start(out=lr_sb[:], in_=lr.rearrange("(p i) o -> p (i o)", i=PACK))
 
         xt_v = xt.rearrange("(a p i) k -> a p i k", p=P, i=PACK)
         gh_v = gh.rearrange("(a p i) r -> a p i r", p=P, i=PACK)
@@ -42,17 +41,24 @@ def tile_list_hot_neuron_wgrad_pl_kernel(tc, xt, gh, mom, lr, offs, out_0, out_1
         y_v = out_0.rearrange("(p i) j -> p i j", i=PACK)
 
         x_raw = [keep.tile([P, PACK, K], F32, name="x_raw%d" % a) for a in range(PASSES)]
-        g_raw = [[keep.tile([P, R], F32, name="g_raw%d_%d" % (a, i)) for i in range(PACK)] for a in range(PASSES)]
+        g_pair = [keep.tile([P, 2, R], F32, name="g_pair%d" % u) for u in range(2)]
+        g_one = [keep.tile([P, R], F32, name="g_one%d" % i) for i in range(PACK)]
+        g_win = [[g_pair[i // 2][:, i % 2, :] for i in range(PACK)], [g_one[i][:] for i in range(PACK)]]
         m_raw = [keep.tile([P, R], F32, name="m_raw%d" % i) for i in range(PACK)]
+        nc.sync.dma_start(out=g_pair[0][:], in_=gh_v[0, :, 0:2, :])
+        nc.sync.dma_start(offsets[:], offs)
+        nc.sync.dma_start(out=g_pair[1][:], in_=gh_v[0, :, 2:4, :])
+        nc.sync.dma_start(out=lr_sb[:], in_=lr.rearrange("(p i) o -> p (i o)", i=PACK))
         for a in range(PASSES):
             nc.sync.dma_start(out=x_raw[a][:], in_=xt_v[a])
-            for i in range(PACK):
-                nc.sync.dma_start(out=g_raw[a][i][:], in_=gh_v[a, :, i, :])
+        for i in range(PACK):
+            nc.sync.dma_start(out=g_one[i][:], in_=gh_v[1, :, i, :])
         for i in range(PACK):
             nc.sync.dma_start(out=m_raw[i][:], in_=mom_v[:, i, :])
 
         step = keep.tile([P, PACK], F32, name="step")
-        nc.vector.tensor_scalar(step[:], lr_sb[:], -1.0 / DECAY, None, MULT)
+        nc.vector.tensor_scalar(step[:, 0:2], lr_sb[:, 0:2], -1.0, None, MULT)
+        nc.vector.tensor_scalar(step[:, 2:4], lr_sb[:, 2:4], -1.0 / DECAY, None, MULT)
 
         acc = [psum.tile([P, J], F32, name="acc%d" % i) for i in range(PACK)]
         for a in range(PASSES):
@@ -63,7 +69,7 @@ def tile_list_hot_neuron_wgrad_pl_kernel(tc, xt, gh, mom, lr, offs, out_0, out_1
             )
             g_bf = keep.tile([P, J, PACK], BF16, name="g_bf%d" % a, align_bytes=64)
             for i in range(PACK):
-                nc.vector.tensor_copy(g_bf[:, :, i], g_raw[a][i][:].indirect(offsets[:]))
+                nc.vector.tensor_copy(g_bf[:, :, i], g_win[a][i].indirect(offsets[:]))
             x_codes = keep.tile([P, K], U32, name="x_codes%d" % a, align_bytes=64)
             x_scales = keep.tile([P, K], U8, name="x_scales%d" % a, align_bytes=64)
             nc.vector.quantize_mx(
@@ -86,37 +92,48 @@ def tile_list_hot_neuron_wgrad_pl_kernel(tc, xt, gh, mom, lr, offs, out_0, out_1
                     stop=(a == PASSES - 1),
                 )
 
-        upd = keep.tile([P, PACK, J], F32, name="upd")
-        for s in range(PACK):
-            nc.scalar.activation(upd[:, s, :], acc[s][:], COPY, scale=step[:, s : s + 1])
-
-        mixed = keep.tile([P, PACK, J], F32, name="mixed")
-        y = keep.tile([P, PACK, J], F32, name="y")
+        halves = [slice(h * HALF, (h + 1) * HALF) for h in range(2)]
         y_bf = [keep.tile([P, HALF, PACK], BF16, name="y_bf%d" % h, align_bytes=64) for h in range(2)]
         y_codes = keep.tile([P, J], U32, name="y_codes", align_bytes=64)
         y_scales = keep.tile([P, J], U8, name="y_scales", align_bytes=64)
-        halves = [slice(h * HALF, (h + 1) * HALF) for h in range(2)]
-        lists = [offsets[:, h * HALF // 16 : (h + 1) * HALF // 16] for h in range(2)]
 
-        def pair_in(first, h):
-            return mixed[:, first : first + 2, halves[h]].rearrange("p i j -> p j i")
-
-        for s in range(PACK - 1):
-            nc.vector.tensor_tensor(mixed[:, s, :], m_raw[s][:].indirect(offsets[:]), upd[:, s, :], ADD)
-            nc.scalar.activation(y[:, s, :], mixed[:, s, :], COPY, scale=DECAY)
-            nc.sync.dma_start(out=y_v[:, s, :], in_=y[:, s, :])
-            if s == 1:
-                for h in range(2):
-                    nc.scalar.activation(y_bf[h][:, :, 0:2], pair_in(0, h), COPY, scale=DECAY)
-        last = PACK - 1
+        picked = keep.tile([P, 2, J], F32, name="picked")
+        y_lo = keep.tile([P, 2, J], F32, name="y_lo")
+        for s in range(2):
+            nc.vector.tensor_scalar(picked[:, s, :], m_raw[s][:].indirect(offsets[:]), DECAY, 0.0, MULT, ADD)
+            nc.vector.scalar_tensor_tensor(y_lo[:, s, :], acc[s][:], step[:, s : s + 1], picked[:, s, :], MULT, ADD)
+        upd = [keep.tile([P, J], F32, name="upd%d" % e) for e in range(2)]
+        for e in range(2):
+            nc.scalar.activation(upd[e][:], acc[2 + e][:], COPY, scale=step[:, 2 + e : 3 + e])
+        nc.sync.dma_start(out=y_v[:, 0:2, :], in_=y_lo[:])
         for h in range(2):
+            nc.scalar.copy(y_bf[h][:, :, 0:2], y_lo[:, :, halves[h]].rearrange("p i j -> p j i"))
+
+        mix_hi = keep.tile([P, 2, J], F32, name="mix_hi")
+        y_2 = keep.tile([P, J], F32, name="y_2")
+        y_3 = [keep.tile([P, HALF], F32, name="y_3%d" % h) for h in range(2)]
+        nc.vector.tensor_tensor(mix_hi[:, 0, :], m_raw[2][:].indirect(offsets[:]), upd[0][:], ADD)
+        nc.scalar.activation(y_2[:], mix_hi[:, 0, :], COPY, scale=DECAY)
+        nc.sync.dma_start(out=y_v[:, 2, :], in_=y_2[:])
+
+        quarters = [slice(q * QUARTER, (q + 1) * QUARTER) for q in range(4)]
+        for q in range(4):
             nc.vector.tensor_tensor(
-                mixed[:, last, halves[h]], m_raw[last][:].indirect(lists[h]), upd[:, last, halves[h]], ADD
+                mix_hi[:, 1, quarters[q]],
+                m_raw[3][:].indirect(offsets[:, q * QUARTER // 16 : (q + 1) * QUARTER // 16]),
+                upd[1][:, quarters[q]],
+                ADD,
             )
-        nc.scalar.activation(y_bf[0][:, :, 2:4], pair_in(2, 0), COPY, scale=DECAY)
-        nc.vector.tensor_scalar(y_bf[1][:, :, 2:4], pair_in(2, 1), DECAY, None, MULT)
-        nc.scalar.activation(y[:, last, :], mixed[:, last, :], COPY, scale=DECAY)
-        nc.sync.dma_start(out=y_v[:, last, :], in_=y[:, last, :])
+        for q in range(4):
+            pair_in = mix_hi[:, :, quarters[q]].rearrange("p i j -> p j i")
+            pair_out = y_bf[q // 2][:, quarters[q % 2], 2:4]
+            if q < 2:
+                nc.scalar.activation(pair_out, pair_in, COPY, scale=DECAY)
+            else:
+                nc.vector.tensor_scalar(pair_out, pair_in, DECAY, None, MULT)
+        for h in range(2):
+            nc.scalar.activation(y_3[h][:], mix_hi[:, 1, halves[h]], COPY, scale=DECAY)
+            nc.scalar.dma_start(out=y_v[:, 3, halves[h]], in_=y_3[h][:])
         words = out_1[0].rearrange("p c r -> p (c r)").bitcast(I32)
         for h in range(2):
             nc.vector.quantize_mx(

from contextlib import ExitStack

import concourse.mybir as mybir

T, K, R, J = 1024, 512, 2048, 512
FLOPS = 2 * T * K * J

F32 = mybir.dt.float32
BF16 = mybir.dt.bfloat16
I32 = mybir.dt.int32
U32 = mybir.dt.uint32
U16 = mybir.dt.uint16
U8 = mybir.dt.uint8
E4M3X4 = mybir.dt.float8_e4m3fn_x4
E5M2X4 = mybir.dt.float8_e5m2_x4
COPY = mybir.ActivationFunctionType.Copy
ADD = mybir.AluOpType.add
MULT = mybir.AluOpType.mult

P = 128
PACK = 4
PASS = P * PACK
PASSES = T // PASS
HALF = J // 2
QUARTER = J // 4
DECAY = 0.9


def tile_list_hot_neuron_wgrad_pl_kernel(tc, xt, gh, mom, lr, offs, out_0, out_1, out_2):
    nc = tc.nc
    with ExitStack() as ctx:
        keep = ctx.enter_context(tc.tile_pool(name="keep", bufs=1))
        psum = ctx.enter_context(tc.psum_pool(name="psum", bufs=1))

        offsets = keep.tile([P, J // 16], U16, name="offsets")
        lr_sb = keep.tile([P, PACK], F32, name="lr_sb")

        xt_v = xt.rearrange("(a p i) k -> a p i k", p=P, i=PACK)
        gh_v = gh.rearrange("(a p i) r -> a p i r", p=P, i=PACK)
        mom_v = mom.rearrange("(p i) r -> p i r", i=PACK)
        y_v = out_0.rearrange("(p i) j -> p i j", i=PACK)

        x_raw = [keep.tile([P, PACK, K], F32, name="x_raw%d" % a) for a in range(PASSES)]
        g_pair = [keep.tile([P, 2, R], F32, name="g_pair%d" % u) for u in range(2)]
        g_one = [keep.tile([P, R], F32, name="g_one%d" % i) for i in range(PACK)]
        g_win = [[g_pair[i // 2][:, i % 2, :] for i in range(PACK)], [g_one[i][:] for i in range(PACK)]]
        m_raw = [keep.tile([P, R], F32, name="m_raw%d" % i) for i in range(PACK)]
        nc.sync.dma_start(out=g_pair[0][:], in_=gh_v[0, :, 0:2, :])
        nc.sync.dma_start(offsets[:], offs)
        nc.sync.dma_start(out=g_pair[1][:], in_=gh_v[0, :, 2:4, :])
        nc.sync.dma_start(out=lr_sb[:], in_=lr.rearrange("(p i) o -> p (i o)", i=PACK))
        for a in range(PASSES):
            nc.sync.dma_start(out=x_raw[a][:], in_=xt_v[a])
        for i in range(PACK):
            nc.sync.dma_start(out=g_one[i][:], in_=gh_v[1, :, i, :])
        for i in range(PACK):
            nc.sync.dma_start(out=m_raw[i][:], in_=mom_v[:, i, :])

        step = keep.tile([P, PACK], F32, name="step")
        nc.vector.tensor_scalar(step[:, 0:2], lr_sb[:, 0:2], -1.0, None, MULT)
        nc.vector.tensor_scalar(step[:, 2:4], lr_sb[:, 2:4], -1.0 / DECAY, None, MULT)

        acc = [psum.tile([P, J], F32, name="acc%d" % i) for i in range(PACK)]
        for a in range(PASSES):
            x_bf = keep.tile([P, PACK, P, PACK], BF16, name="x_bf%d" % a, align_bytes=64)
            nc.scalar.copy(
                out=x_bf[:].rearrange("p s m i -> p m s i"),
                in_=x_raw[a][:].rearrange("p i (m s) -> p m s i", s=PACK),
            )
            g_bf = keep.tile([P, J, PACK], BF16, name="g_bf%d" % a, align_bytes=64)
            for i in range(PACK):
                nc.vector.tensor_copy(g_bf[:, :, i], g_win[a][i].indirect(offsets[:]))
            x_codes = keep.tile([P, K], U32, name="x_codes%d" % a, align_bytes=64)
            x_scales = keep.tile([P, K], U8, name="x_scales%d" % a, align_bytes=64)
            nc.vector.quantize_mx(
                out=x_codes[:].bitcast(E4M3X4), scales=x_scales[:], in_=x_bf[:].rearrange("p s m i -> p (s m i)")
            )
            g_codes = keep.tile([P, J], U32, name="g_codes%d" % a, align_bytes=64)
            g_scales = keep.tile([P, J], U8, name="g_scales%d" % a, align_bytes=64)
            nc.vector.quantize_mx(
                out=g_codes[:].bitcast(E5M2X4), scales=g_scales[:], in_=g_bf[:].rearrange("p j i -> p (j i)")
            )
            for s in range(PACK):
                cols = slice(s * P, (s + 1) * P)
                nc.tensor.matmul_mx(
                    out=acc[s][:],
                    lhsT=x_codes[:, cols].bitcast(E4M3X4),
                    lhsT_scale=x_scales[:, cols],
                    rhs=g_codes[:].bitcast(E5M2X4),
                    rhs_scale=g_scales[:],
                    start=(a == 0),
                    stop=(a == PASSES - 1),
                )

        halves = [slice(h * HALF, (h + 1) * HALF) for h in range(2)]
        y_bf = [keep.tile([P, HALF, PACK], BF16, name="y_bf%d" % h, align_bytes=64) for h in range(2)]
        y_codes = keep.tile([P, J], U32, name="y_codes", align_bytes=64)
        y_scales = keep.tile([P, J], U8, name="y_scales", align_bytes=64)

        picked = keep.tile([P, 2, J], F32, name="picked")
        y_lo = keep.tile([P, 2, J], F32, name="y_lo")
        for s in range(2):
            nc.vector.tensor_scalar(picked[:, s, :], m_raw[s][:].indirect(offsets[:]), DECAY, 0.0, MULT, ADD)
            nc.vector.scalar_tensor_tensor(y_lo[:, s, :], acc[s][:], step[:, s : s + 1], picked[:, s, :], MULT, ADD)
        upd = [keep.tile([P, J], F32, name="upd%d" % e) for e in range(2)]
        for e in range(2):
            nc.scalar.activation(upd[e][:], acc[2 + e][:], COPY, scale=step[:, 2 + e : 3 + e])
        nc.sync.dma_start(out=y_v[:, 0:2, :], in_=y_lo[:])
        for h in range(2):
            nc.scalar.copy(y_bf[h][:, :, 0:2], y_lo[:, :, halves[h]].rearrange("p i j -> p j i"))

        mix_hi = keep.tile([P, 2, J], F32, name="mix_hi")
        y_2 = keep.tile([P, J], F32, name="y_2")
        y_3 = [keep.tile([P, HALF], F32, name="y_3%d" % h) for h in range(2)]
        nc.vector.tensor_tensor(mix_hi[:, 0, :], m_raw[2][:].indirect(offsets[:]), upd[0][:], ADD)
        nc.scalar.activation(y_2[:], mix_hi[:, 0, :], COPY, scale=DECAY)
        nc.sync.dma_start(out=y_v[:, 2, :], in_=y_2[:])

        quarters = [slice(q * QUARTER, (q + 1) * QUARTER) for q in range(4)]
        for q in range(4):
            nc.vector.tensor_tensor(
                mix_hi[:, 1, quarters[q]],
                m_raw[3][:].indirect(offsets[:, q * QUARTER // 16 : (q + 1) * QUARTER // 16]),
                upd[1][:, quarters[q]],
                ADD,
            )
        for q in range(4):
            pair_in = mix_hi[:, :, quarters[q]].rearrange("p i j -> p j i")
            pair_out = y_bf[q // 2][:, quarters[q % 2], 2:4]
            if q < 2:
                nc.scalar.activation(pair_out, pair_in, COPY, scale=DECAY)
            else:
                nc.vector.tensor_scalar(pair_out, pair_in, DECAY, None, MULT)
        for h in range(2):
            nc.scalar.activation(y_3[h][:], mix_hi[:, 1, halves[h]], COPY, scale=DECAY)
            nc.scalar.dma_start(out=y_v[:, 3, halves[h]], in_=y_3[h][:])
        words = out_1[0].rearrange("p c r -> p (c r)").bitcast(I32)
        for h in range(2):
            nc.vector.quantize_mx(
                out=y_codes[:, halves[h]].bitcast(E4M3X4),
                scales=y_scales[:, halves[h]],
                in_=y_bf[h][:].rearrange("p j i -> p (j i)"),
            )
            nc.sync.dma_start(out=words[:, halves[h]], in_=y_codes[:, halves[h]].bitcast(I32))
        scale_rows = out_2[0].bitcast(I32)
        for q in range(4):
            queue = nc.scalar if q % 2 == 0 else nc.sync
            queue.dma_start(out=scale_rows[4 * q : 4 * q + 4, :], in_=y_scales[32 * q : 32 * q + 4, :].bitcast(I32))
